import numpy as np, ml_dtypes
CORES = [100,101,102,103,108,109,110,111]
N = 8
NH, QP = 8, 128
def setup_inputs(rng):
    q = rng.standard_normal((N, 128, NH * QP), dtype=np.float32) / 4; k = rng.standard_normal((N, 128, NH * 128), dtype=np.float32)
    a = 2 * np.pi * rng.random((N, NH * QP)); s = 400 * rng.random((N, NH * QP)) ** 1.5; q[:, 0, :] = s * np.cos(a); q[:, 1, :] = s * np.sin(a); q[:, 2, :] = 150 * rng.standard_normal((N, NH * QP)); k[:, 2, :] = 1 + k[:, 2, :] / 50
    a = (2 * np.pi * rng.random((1, NH, 1)) + np.pi / 2 * (rng.permuted(np.tile(np.arange(N), (NH, 1)), axis=1).T.reshape(N, NH, 1) + 0.5) / N - 0.5 + rng.random((N, NH, 128))).reshape(N, NH * 128); k[:, 0, :] = np.cos(a); k[:, 1, :] = np.sin(a)
    return {"q": q.astype(ml_dtypes.bfloat16), "k": k.astype(ml_dtypes.bfloat16), "v": rng.standard_normal((N, 128, NH * 128), dtype=np.float32).astype(ml_dtypes.bfloat16)}
def setup_inputs_big(rng):
    d = setup_inputs(rng)
    for k in ("v",): d[k] = (d[k].astype(np.float32) * 1048576.0).astype(d[k].dtype)
    return d
def setup_inputs_small(rng):
    d = setup_inputs(rng)
    for k in ("v",): d[k] = (d[k].astype(np.float32) * (1 / 1048576.0)).astype(d[k].dtype)
    return d
def reference(q, k, v):
    Q, K, V = q.astype(np.float64), k.astype(np.float64), v.astype(np.float64)
    y = np.zeros((N, QP, NH * 128))
    for r in range(N):
        for h in range(NH):
            S = np.concatenate([K[j][:, 128 * h:128 * h + 128].T @ Q[r][:, QP * h:QP * h + QP] for j in range(N)], axis=0)
            P = np.exp(S - S.max(axis=0)); P = P / P.sum(axis=0)
            y[r][:, 128 * h:128 * h + 128] = P.T @ np.concatenate([V[j][:, 128 * h:128 * h + 128] for j in range(N)], axis=0)
    return {"y": y.astype(ml_dtypes.bfloat16)}

@@ -1,0 +1,345 @@
+from concourse.bass import DstId, RemoteDMATransfer
+from concourse.mybir import AluOpType, AxisListType, ActivationFunctionType
+
+NH = 8
+B = 128
+GW = 3 * B
+NS, NP, NT, ND = 3, 4, 3, 4
+
+SCRATCH = {
+    "KVn": ("sbuf", [128, 2 * NH * B], "bfloat16"),
+    "Qn": ("sbuf", [128, NH * B], "bfloat16"),
+    "X": ("sbuf", [128, NH * GW], "bfloat16"),
+    "L": ("sbuf", [128, 4 * GW], "bfloat16"),
+    "R": ("sbuf", [128, 4 * 2 * B], "bfloat16"),
+    "ones": ("sbuf", [128, B], "bfloat16"),
+    "ident": ("sbuf", [128, B], "bfloat16"),
+    "P": ("sbuf", [128, NP * 512], "bfloat16"),
+    "PTs": ("sbuf", [128, NT * 512], "bfloat16"),
+    "D": ("sbuf", [128, ND * B], "bfloat16"),
+    "Orun": ("sbuf", [128, 4 * B], "bfloat16"),
+    "Yo": ("sbuf", [128, 4 * B], "bfloat16"),
+    "Y": ("sbuf", [128, NH * B], "bfloat16"),
+    "ST": ("sbuf", [128, 96], "float32"),
+    "S0": ("psum", [128, 512], "float32"),
+    "S1": ("psum", [128, 512], "float32"),
+    "S2": ("psum", [128, 512], "float32"),
+    "PT0": ("psum", [128, 1024], "bfloat16"),
+    "PT1": ("psum", [128, 1024], "bfloat16"),
+    "O0": ("psum", [128, 512], "float32"),
+    "O1": ("psum", [128, 512], "float32"),
+}
+SEMAPHORES = ["pe", "ve", "se", "gp", "ldk", "ldv", "ldq", "feed", "arrL", "arrD", "arrR", "yarr", "snd", "st"]
+
+
+def _bits(m):
+    return [e for e in range(m.bit_length()) if (m >> e) & 1]
+
+
+def _mask(es):
+    return sum(1 << e for e in es)
+
+
+def _plan(T, topo):
+    ranks = [int(c) for c in T.cores]
+    chips = []
+    for c in ranks:
+        if topo.chip(c) not in chips:
+            chips.append(topo.chip(c))
+    allc = range(topo.CHIPS * topo.CORES_PER_CHIP)
+    members = {ch: [c for c in allc if topo.chip(c) == ch] for ch in chips}
+    loc = {ch: [c for c in ranks if topo.chip(c) == ch] for ch in chips}
+    other = {chips[0]: chips[1], chips[1]: chips[0]}
+    carrier = {}
+    for ch in chips:
+        far = members[other[ch]][0]
+        own_dies = [topo.die(r) for r in loc[ch] if topo.may_write(r, far)]
+        free = [c for c in members[ch] if c not in ranks and topo.may_write(c, far)]
+        free.sort(key=lambda c: topo.die(c) in own_dies)
+        for r in loc[ch]:
+            carrier[r] = r if topo.may_write(r, far) else free.pop(0)
+    return {"members": members, "loc": loc, "other": other, "carrier": carrier}
+
+
+def rank_program(g, core, T, topo):
+    pl = _plan(T, topo)
+    ch = topo.chip(core)
+    if ch not in pl["members"]:
+        return
+    members, loc = pl["members"][ch], pl["loc"][ch]
+    far_members, far_loc = pl["members"][pl["other"][ch]], pl["loc"][pl["other"][ch]]
+    carrier = pl["carrier"]
+    h = members.index(core)
+    is_rank = core in loc
+    carried = [r for r in loc if carrier[r] == core]
+    Act, Alu = ActivationFunctionType, AluOpType
+
+    queues = {"pe": g.tensor, "ve": g.vector, "se": g.scalar, "gp": g, "sy": g.sync}
+    cnt = {"pe": 0, "ve": 0, "se": 0, "gp": 0}
+    seen = {q: {} for q in queues}
+    expect = {}
+    sent = [0]
+
+    def need(q, deps):
+        for d in deps:
+            if d is not None and seen[q].get(d[0], 0) < d[1]:
+                queues[q].wait_ge(T.sem[d[0]], d[1])
+                seen[q][d[0]] = d[1]
+
+    def emit(q, deps, fn):
+        need(q, deps)
+        fn().then_inc(T.sem[q], 1)
+        cnt[q] += 1
+        return (q, cnt[q])
+
+    def dst_id(c):
+        rid, pid, _se = topo.addr(c)
+        return DstId(rid=rid, pnc=pid)
+
+    def col(t, j, w=B):
+        return t[:, j * w:(j + 1) * w]
+
+    X = T.X
+    xk = lambda hh: X[:, GW * hh:GW * hh + B]
+    xv = lambda hh: X[:, GW * hh + B:GW * hh + 2 * B]
+    xq = lambda hh: X[:, GW * hh + 2 * B:GW * hh + 3 * B]
+    nk = lambda hh: T.KVn[:, B * hh:B * hh + B]
+    nv = lambda hh: T.KVn[:, NH * B + B * hh:NH * B + B * hh + B]
+
+    if is_rank:
+        g.sync.dma_start(T.KVn[:, 0:NH * B], T.k[:]).then_inc(T.sem.ldk, 16)
+        g.scalar.dma_start(T.KVn[:, NH * B:2 * NH * B], T.v[:]).then_inc(T.sem.ldv, 16)
+        g.sync.dma_start(T.Qn[:], T.q[:]).then_inc(T.sem.ldq, 16)
+        expect.update({"ldk": 16, "ldv": 16, "ldq": 16})
+
+    t_ones = emit("ve", [], lambda: g.vector.memset(T.ones[:], 1.0))
+    t_id = emit("gp", [t_ones], lambda: g.affine_select(T.ident[:], T.ones[:], [[-1, B]], Alu.is_equal, 0.0, 0, 1))
+
+    if is_rank and carrier[core] != core:
+        c = carrier[core]
+        m = topo.mask(core, c)
+        rid, pid, _se = topo.addr(c)
+        need("gp", [("ldk", 16), ("ldv", 16)])
+        g.remote_dma(T.KVn[:], T.KVn[:], T.sem.feed, T.sem.snd, pid, rid, m)
+        sent[0] += len(_bits(m))
+
+    il = []
+    if is_rank:
+        for hh in range(NH):
+            tv = emit("ve", [("ldk", 16)], lambda: g.vector.tensor_copy(xk(hh), nk(hh)))
+        for hh in range(NH):
+            tv = emit("ve", [("ldv", 16)], lambda: g.vector.tensor_copy(xv(hh), nv(hh)))
+        for hh in range(NH):
+            ts = emit("se", [("ldq", 16)], lambda: g.scalar.activation(xq(hh), col(T.Qn, hh), Act.Copy))
+        il = [tv, ts]
+    elif carried:
+        nfeed = len(_bits(topo.mask(carried[0], core)))
+        expect["feed"] = nfeed
+        jobs = [(xk(hh), nk(hh)) for hh in range(NH)] + [(xv(hh), nv(hh)) for hh in range(NH)]
+        nve = (2 * len(jobs) + 2) // 3
+        for o, i in jobs[:nve]:
+            tv = emit("ve", [("feed", nfeed)], lambda: g.vector.tensor_copy(o, i))
+        for o, i in jobs[nve:]:
+            ts = emit("se", [("feed", nfeed)], lambda: g.scalar.activation(o, i, Act.Copy))
+        il = [tv, ts]
+
+    def scatter_masks(src):
+        ds = [w for w in members if w != src]
+        ds.sort(key=lambda w: topo.die(w) == topo.die(src))
+        es = _bits(topo.mask(src, ds[0]))
+        pool = es[0::2] + es[1::2]
+        per = 1
+        while per * 2 * len(ds) <= len(pool):
+            per *= 2
+        return {w: pool[per * i:per * i + per] for i, w in enumerate(ds)}
+
+    if is_rank:
+        need("gp", il)
+        sm = scatter_masks(core)
+        b = loc.index(core)
+        trs = [RemoteDMATransfer(dst_ids=[dst_id(w)], dma_engine_mask=_mask(es), remote_sem=T.sem.arrL,
+                                 src=col(X, members.index(w), GW), dst=col(T.L, b, GW)) for w, es in sm.items()]
+        g.remote_dma_fused(trs, local_sem=T.sem.snd)
+        sent[0] += sum(len(es) for es in sm.values())
+    nL = sum(len(scatter_masks(r)[core]) for r in loc if r != core)
+    expect["arrL"] = nL
+
+    if carried:
+        need("gp", il)
+        r = carried[0]
+        b = loc.index(r)
+        es = _bits(topo.mask(core, far_members[0]))
+        per = len(es) // NH
+        sem = T.sem.arrD if r == core else T.sem.arrR
+        trs = [RemoteDMATransfer(dst_ids=[dst_id(w)], dma_engine_mask=_mask(es[per * i:per * i + per]), remote_sem=sem,
+                                 src=X[:, GW * i:GW * i + 2 * B], dst=col(T.R, b, 2 * B)) for i, w in enumerate(far_members)]
+        g.remote_dma_fused(trs, local_sem=T.sem.snd)
+        sent[0] += per * NH
+    per_far = len(_bits(topo.mask(far_members[0], core))) // NH
+    far_d = [r for r in far_loc if carrier[r] == r]
+    far_r = [r for r in far_loc if carrier[r] != r]
+    expect["arrD"] = per_far * len(far_d)
+    expect["arrR"] = per_far * len(far_r)
+
+    q_ap, kv_loc = [], []
+    for b, r in enumerate(loc):
+        if r == core:
+            q_ap.append(xq(h))
+            kv_loc.append((xk(h), xv(h)))
+        else:
+            o = GW * b
+            q_ap.append(T.L[:, o + 2 * B:o + 3 * B])
+            kv_loc.append((T.L[:, o:o + B], T.L[:, o + B:o + 2 * B]))
+
+    def kv_far(r):
+        o = 2 * B * far_loc.index(r)
+        return (T.R[:, o:o + B], T.R[:, o + B:o + 2 * B])
+
+    stages = [(kv_loc, [("arrL", nL)] + il)]
+    if far_d:
+        stages.append(([kv_far(r) for r in far_d], [("arrD", expect["arrD"])]))
+    if far_r:
+        stages.append(([kv_far(r) for r in far_r], [("arrR", expect["arrR"])]))
+
+    nb = len(loc)
+    order = [(h + 1 + j) % nb for j in range(nb)]
+    Sb = [T.S0, T.S1, T.S2]
+    PTp = [T.PT0, T.PT1]
+    Ob = [T.O0, T.O1]
+    stc = [0]
+
+    def newcol():
+        stc[0] += 1
+        return T.ST[:, stc[0] - 1:stc[0]]
+
+    tok = {}
+    run = {b: {} for b in range(nb)}
+    it = {}
+    ret_es = None
+    y_own = [None]
+
+    def do_S(i, b, ck, deps):
+        for c, (k, _v) in enumerate(ck):
+            t = emit("pe", deps + [tok.get(("exp", i - NS))], lambda: g.tensor.matmul(col(Sb[i % NS], c), q_ap[b], k, True, True))
+        tok[("S", i)] = t
+
+    def do_MAX(i, b, ck, first):
+        w = B * len(ck)
+        nm = newcol()
+        t = emit("ve", [tok[("S", i)]], lambda: g.vector.tensor_reduce(nm, Sb[i % NS][:, 0:w], AxisListType.X, Alu.max, negate=True))
+        d = {"old": None}
+        if not first:
+            ng = newcol()
+            old = run[b]["ng"]
+            t = emit("ve", [t, run[b]["t_ng"]], lambda: g.vector.tensor_tensor(ng, nm, old, Alu.min))
+            d["old"] = old
+            nm = ng
+        d["ng"] = nm
+        run[b]["ng"], run[b]["t_ng"] = nm, t
+        it[i] = d
+
+    def do_EXP(i, b, ck, first):
+        w = B * len(ck)
+        d = it[i]
+        if not first:
+            d["al"] = newcol()
+            d["t_al"] = emit("se", [run[b]["t_ng"]], lambda: g.scalar.activation(d["al"], d["old"], Act.Exp, bias=d["ng"], scale=-1.0))
+        d["ls"] = newcol()
+        p = T.P[:, 512 * (i % NP):512 * (i % NP) + w]
+        tok[("exp", i)] = emit("se", [run[b]["t_ng"], tok.get(("T", i - NP))],
+                               lambda: g.scalar.activation(p, Sb[i % NS][:, 0:w], Act.Exp, bias=d["ng"], scale=1.0, accum_out=d["ls"]))
+
+    def do_T(i, ck):
+        for c in range(len(ck)):
+            t = emit("pe", [tok[("exp", i)], tok.get(("cp", i - 2)), t_id],
+                     lambda: g.tensor.transpose(col(PTp[i % 2], c), col(T.P, 4 * (i % NP) + c), T.ident[:]))
+        tok[("T", i)] = t
+
+    def do_PRE(i, b, first, last):
+        d = it[i]
+        if first:
+            run[b]["l"], run[b]["t_l"] = d["ls"], tok[("exp", i)]
+        else:
+            d["t_D"] = emit("ve", [d["t_al"], t_id, tok.get(("pv", i - ND))],
+                            lambda: g.vector.tensor_scalar(col(T.D, i % ND), T.ident[:], d["al"], None, Alu.mult))
+            ln, lo = newcol(), run[b]["l"]
+            t = emit("ve", [d["t_al"], tok[("exp", i)], run[b]["t_l"]],
+                     lambda: g.vector.tensor_scalar(ln, lo, d["al"], d["ls"], Alu.mult, Alu.add))
+            run[b]["l"], run[b]["t_l"] = ln, t
+        if last:
+            d["rl"] = newcol()
+            d["t_rl"] = emit("ve", [run[b]["t_l"]], lambda: g.vector.reciprocal(d["rl"], run[b]["l"]))
+
+    def do_CP(i, ck):
+        w = B * len(ck)
+        o = 512 * (i % NT)
+        tok[("cp", i)] = emit("ve", [tok[("T", i)], tok.get(("pv", i - NT))],
+                              lambda: g.vector.tensor_copy(T.PTs[:, o:o + w], PTp[i % 2][:, 0:w]))
+
+    def do_PV(i, b, ck, first):
+        out = Ob[i % 2][:, 0:B]
+        deps = [tok[("cp", i)], tok.get(("out", i - 2))]
+        if not first:
+            emit("pe", deps + [it[i]["t_D"], run[b]["t_O"]], lambda: g.tensor.matmul(out, col(T.D, i % ND), col(T.Orun, b), True, False))
+        for c, (_k, v) in enumerate(ck):
+            t = emit("pe", deps, lambda: g.tensor.matmul(out, col(T.PTs, 4 * (i % NT) + c), v, first and c == 0, c == len(ck) - 1))
+        tok[("pv", i)] = t
+
+    def do_OUT(i, b, last):
+        src = Ob[i % 2][:, 0:B]
+        if not last:
+            t = emit("ve", [tok[("pv", i)]], lambda: g.vector.tensor_copy(col(T.Orun, b), src))
+            run[b]["t_O"] = t
+        else:
+            own = loc[b] == core
+            o = col(T.Y, h) if own else col(T.Yo, b)
+            t = emit("ve", [tok[("pv", i)], it[i]["t_rl"]], lambda: g.vector.tensor_scalar(o, src, it[i]["rl"], None, Alu.mult))
+            if own:
+                y_own[0] = t
+            else:
+                es = _bits(topo.mask(core, loc[b]))[0::2]
+                rid, pid, _se = topo.addr(loc[b])
+                need("gp", [t])
+                g.remote_dma(col(T.Y, h), col(T.Yo, b), T.sem.yarr, T.sem.snd, pid, rid, _mask(es))
+                sent[0] += len(es)
+        tok[("out", i)] = t
+
+    i0 = 0
+    for s, (ck, deps) in enumerate(stages):
+        first, last = s == 0, s == len(stages) - 1
+
+        def head(j):
+            do_S(i0 + j, order[j], ck, deps)
+            do_MAX(i0 + j, order[j], ck, first)
+            do_EXP(i0 + j, order[j], ck, first)
+
+        def mid(j):
+            do_T(i0 + j, ck)
+            do_PRE(i0 + j, order[j], first, last)
+            do_CP(i0 + j, ck)
+
+        def tail(j):
+            do_PV(i0 + j, order[j], ck, first)
+            do_OUT(i0 + j, order[j], last)
+
+        for j in range(min(NS, nb)):
+            head(j)
+        for j in range(nb):
+            mid(j)
+            if j + NS < nb:
+                head(j + NS)
+            if j >= 1:
+                tail(j - 1)
+        tail(nb - 1)
+        i0 += nb
+
+    if is_rank:
+        ny = sum(len(_bits(topo.mask(w, core))[0::2]) for w in members if w != core)
+        expect["yarr"] = ny
+        need("sy", [("yarr", ny), y_own[0]])
+        g.sync.dma_start(T.y[:], T.Y[:]).then_inc(T.sem.st, 16)
+        expect["st"] = 16
+
+    expect["snd"] = sent[0]
+    expect.update(cnt)
+    need("gp", [(s, n) for s, n in expect.items() if n > 0])

@@ -4,7 +4,9 @@ from concourse.mybir import AluOpType, AxisListType, ActivationFunctionType
 NH = 8
 B = 128
 GW = 3 * B
-NS, NP, NT, ND = 3, 4, 3, 4
+NG = 2
+HG = NH // NG
+NS, NP, NT, ND = 4, 4, 3, 4
 
 SCRATCH = {
     "KVn": ("sbuf", [128, 2 * NH * B], "bfloat16"),
@@ -24,12 +26,14 @@ SCRATCH = {
     "S0": ("psum", [128, 512], "float32"),
     "S1": ("psum", [128, 512], "float32"),
     "S2": ("psum", [128, 512], "float32"),
+    "S3": ("psum", [128, 512], "float32"),
     "PT0": ("psum", [128, 1024], "bfloat16"),
     "PT1": ("psum", [128, 1024], "bfloat16"),
     "O0": ("psum", [128, 512], "float32"),
     "O1": ("psum", [128, 512], "float32"),
 }
-SEMAPHORES = ["pe", "ve", "se", "gp", "ldk", "ldv", "ldq", "feed", "arrL", "arrD", "arrR", "yarr", "snd", "st"]
+SEMAPHORES = ["pe", "ve", "se", "gp", "lk0", "lv0", "lq0", "lk1", "lv1", "lq1", "feed0", "feed1",
+              "arrL", "arrD", "arrR", "yarr0", "yarr1", "snd", "st0", "st1"]
 
 
 def _bits(m):
@@ -100,86 +104,108 @@ def rank_program(g, core, T, topo):
         return t[:, j * w:(j + 1) * w]
 
     X = T.X
+    GB = HG * B
     xk = lambda hh: X[:, GW * hh:GW * hh + B]
     xv = lambda hh: X[:, GW * hh + B:GW * hh + 2 * B]
     xq = lambda hh: X[:, GW * hh + 2 * B:GW * hh + 3 * B]
-    nk = lambda hh: T.KVn[:, B * hh:B * hh + B]
-    nv = lambda hh: T.KVn[:, NH * B + B * hh:NH * B + B * hh + B]
+    nk = lambda hh: col(T.KVn, 2 * HG * (hh // HG) + hh % HG)
+    nv = lambda hh: col(T.KVn, 2 * HG * (hh // HG) + HG + hh % HG)
 
     if is_rank:
-        g.sync.dma_start(T.KVn[:, 0:NH * B], T.k[:]).then_inc(T.sem.ldk, 16)
-        g.scalar.dma_start(T.KVn[:, NH * B:2 * NH * B], T.v[:]).then_inc(T.sem.ldv, 16)
-        g.sync.dma_start(T.Qn[:], T.q[:]).then_inc(T.sem.ldq, 16)
-        expect.update({"ldk": 16, "ldv": 16, "ldq": 16})
+        jobs = []
+        for gi in range(NG):
+            jobs.append((T.KVn[:, 2 * GB * gi:2 * GB * gi + GB], col(T.k, gi, GB), "lk%d" % gi))
+            jobs.append((T.KVn[:, 2 * GB * gi + GB:2 * GB * gi + 2 * GB], col(T.v, gi, GB), "lv%d" % gi))
+            jobs.append((col(T.Qn, gi, GB), col(T.q, gi, GB), "lq%d" % gi))
+        for n, (o, i, s) in enumerate(jobs):
+            (g.sync if n % 2 == 0 else g.scalar).dma_start(o, i).then_inc(T.sem[s], 16)
+            expect[s] = 16
 
     t_ones = emit("ve", [], lambda: g.vector.memset(T.ones[:], 1.0))
     t_id = emit("gp", [t_ones], lambda: g.affine_select(T.ident[:], T.ones[:], [[-1, B]], Alu.is_equal, 0.0, 0, 1))
 
-    if is_rank and carrier[core] != core:
-        c = carrier[core]
-        m = topo.mask(core, c)
-        rid, pid, _se = topo.addr(c)
-        need("gp", [("ldk", 16), ("ldv", 16)])
-        g.remote_dma(T.KVn[:], T.KVn[:], T.sem.feed, T.sem.snd, pid, rid, m)
-        sent[0] += len(_bits(m))
-
-    il = []
-    if is_rank:
-        for hh in range(NH):
-            tv = emit("ve", [("ldk", 16)], lambda: g.vector.tensor_copy(xk(hh), nk(hh)))
-        for hh in range(NH):
-            tv = emit("ve", [("ldv", 16)], lambda: g.vector.tensor_copy(xv(hh), nv(hh)))
-        for hh in range(NH):
-            ts = emit("se", [("ldq", 16)], lambda: g.scalar.activation(xq(hh), col(T.Qn, hh), Act.Copy))
-        il = [tv, ts]
-    elif carried:
-        nfeed = len(_bits(topo.mask(carried[0], core)))
-        expect["feed"] = nfeed
-        jobs = [(xk(hh), nk(hh)) for hh in range(NH)] + [(xv(hh), nv(hh)) for hh in range(NH)]
-        nve = (2 * len(jobs) + 2) // 3
-        for o, i in jobs[:nve]:
-            tv = emit("ve", [("feed", nfeed)], lambda: g.vector.tensor_copy(o, i))
-        for o, i in jobs[nve:]:
-            ts = emit("se", [("feed", nfeed)], lambda: g.scalar.activation(o, i, Act.Copy))
-        il = [tv, ts]
-
-    def scatter_masks(src):
-        ds = [w for w in members if w != src]
-        ds.sort(key=lambda w: topo.die(w) == topo.die(src))
-        es = _bits(topo.mask(src, ds[0]))
-        pool = es[0::2] + es[1::2]
+    def scatter_masks(src, gi):
+        ds = [members[hh] for hh in range(HG * gi, HG * gi + HG) if members[hh] != src]
+        pool = _bits(topo.mask(src, ds[0]))
+        if gi > 0 and carrier[src] == src:
+            out = _bits(topo.mask(src, far_members[0]))
+            pool = [e for e in pool if e not in out]
         per = 1
         while per * 2 * len(ds) <= len(pool):
             per *= 2
         return {w: pool[per * i:per * i + per] for i, w in enumerate(ds)}
 
-    if is_rank:
-        need("gp", il)
-        sm = scatter_masks(core)
-        b = loc.index(core)
-        trs = [RemoteDMATransfer(dst_ids=[dst_id(w)], dma_engine_mask=_mask(es), remote_sem=T.sem.arrL,
-                                 src=col(X, members.index(w), GW), dst=col(T.L, b, GW)) for w, es in sm.items()]
-        g.remote_dma_fused(trs, local_sem=T.sem.snd)
-        sent[0] += sum(len(es) for es in sm.values())
-    nL = sum(len(scatter_masks(r)[core]) for r in loc if r != core)
-    expect["arrL"] = nL
+    off = _bits(topo.mask(core, far_members[0]))
+    per_off = len(off) // HG
+    il = {}
 
-    if carried:
-        need("gp", il)
+    def carrier_regroup(gi):
+        hs = range(HG * gi, HG * gi + HG)
+        fd = ("feed%d" % gi, len(_bits(topo.mask(carried[0], core))))
+        expect[fd[0]] = fd[1]
+        jobs = [(xk(hh), nk(hh)) for hh in hs] + [(xv(hh), nv(hh)) for hh in hs]
+        nve = (2 * len(jobs) + 2) // 3 if gi == 0 else len(jobs)
+        ts = None
+        for o, i in jobs[:nve]:
+            tv = emit("ve", [fd], lambda: g.vector.tensor_copy(o, i))
+        for o, i in jobs[nve:]:
+            ts = emit("se", [fd], lambda: g.scalar.activation(o, i, Act.Copy))
+        il[gi] = [tv, ts]
+
+    def cross(gi):
+        need("gp", il[gi])
         r = carried[0]
         b = loc.index(r)
-        es = _bits(topo.mask(core, far_members[0]))
-        per = len(es) // NH
         sem = T.sem.arrD if r == core else T.sem.arrR
-        trs = [RemoteDMATransfer(dst_ids=[dst_id(w)], dma_engine_mask=_mask(es[per * i:per * i + per]), remote_sem=sem,
-                                 src=X[:, GW * i:GW * i + 2 * B], dst=col(T.R, b, 2 * B)) for i, w in enumerate(far_members)]
+        trs = [RemoteDMATransfer(dst_ids=[dst_id(far_members[hh])], dma_engine_mask=_mask(off[per_off * i:per_off * i + per_off]),
+                                 remote_sem=sem, src=X[:, GW * hh:GW * hh + 2 * B], dst=col(T.R, b, 2 * B))
+               for i, hh in enumerate(range(HG * gi, HG * gi + HG))]
         g.remote_dma_fused(trs, local_sem=T.sem.snd)
-        sent[0] += per * NH
-    per_far = len(_bits(topo.mask(far_members[0], core))) // NH
+        sent[0] += per_off * HG
+
+    later = []
+    for gi in range(NG):
+        hs = range(HG * gi, HG * gi + HG)
+        lk, lv, lq = ("lk%d" % gi, 16), ("lv%d" % gi, 16), ("lq%d" % gi, 16)
+        if is_rank and carrier[core] != core:
+            c = carrier[core]
+            m = topo.mask(core, c)
+            rid, pid, _se = topo.addr(c)
+            need("gp", [lk, lv])
+            g.remote_dma(col(T.KVn, gi, 2 * GB), col(T.KVn, gi, 2 * GB), T.sem["feed%d" % gi], T.sem.snd, pid, rid, m)
+            sent[0] += len(_bits(m))
+        if is_rank:
+            for hh in hs:
+                tv = emit("ve", [lk], lambda: g.vector.tensor_copy(xk(hh), nk(hh)))
+            for hh in hs:
+                tv = emit("ve", [lv], lambda: g.vector.tensor_copy(xv(hh), nv(hh)))
+            for hh in hs[:HG // 2]:
+                ts = emit("se", [lq], lambda: g.scalar.activation(xq(hh), col(T.Qn, hh), Act.Copy))
+            for hh in hs[HG // 2:]:
+                tv = emit("ve", [lq], lambda: g.vector.tensor_copy(xq(hh), col(T.Qn, hh)))
+            il[gi] = [tv, ts]
+            need("gp", il[gi])
+            sm = scatter_masks(core, gi)
+            b = loc.index(core)
+            trs = [RemoteDMATransfer(dst_ids=[dst_id(w)], dma_engine_mask=_mask(es), remote_sem=T.sem.arrL,
+                                     src=col(X, members.index(w), GW), dst=col(T.L, b, GW)) for w, es in sm.items()]
+            g.remote_dma_fused(trs, local_sem=T.sem.snd)
+            sent[0] += sum(len(es) for es in sm.values())
+            if carried:
+                cross(gi)
+        elif carried:
+            if gi == 0:
+                carrier_regroup(gi)
+                cross(gi)
+            else:
+                later.append(gi)
+
+    nL = sum(len(scatter_masks(r, h // HG)[core]) for r in loc if r != core)
     far_d = [r for r in far_loc if carrier[r] == r]
     far_r = [r for r in far_loc if carrier[r] != r]
-    expect["arrD"] = per_far * len(far_d)
-    expect["arrR"] = per_far * len(far_r)
+    expect["arrL"] = nL
+    expect["arrD"] = per_off * len(far_d)
+    expect["arrR"] = per_off * len(far_r)
 
     q_ap, kv_loc = [], []
     for b, r in enumerate(loc):
@@ -195,15 +221,17 @@ def rank_program(g, core, T, topo):
         o = 2 * B * far_loc.index(r)
         return (T.R[:, o:o + B], T.R[:, o + B:o + 2 * B])
 
-    stages = [(kv_loc, [("arrL", nL)] + il)]
-    if far_d:
-        stages.append(([kv_far(r) for r in far_d], [("arrD", expect["arrD"])]))
-    if far_r:
-        stages.append(([kv_far(r) for r in far_r], [("arrR", expect["arrR"])]))
+    stages = [(kv_loc, [("arrL", nL)] + (il[h // HG] if is_rank else []))]
+    far_st = [([kv_far(r) for r in rs], [(s, expect[s])]) for rs, s in ((far_d, "arrD"), (far_r, "arrR")) if rs]
+    if is_rank:
+        stages += far_st
+    else:
+        stages.append((sum([c for c, _d in far_st], []), sum([d for _c, d in far_st], [])))
+    nst = len(stages)
 
     nb = len(loc)
     order = [(h + 1 + j) % nb for j in range(nb)]
-    Sb = [T.S0, T.S1, T.S2]
+    Sb = [T.S0, T.S1, T.S2, T.S3]
     PTp = [T.PT0, T.PT1]
     Ob = [T.O0, T.O1]
     stc = [0]
@@ -215,7 +243,6 @@ def rank_program(g, core, T, topo):
     tok = {}
     run = {b: {} for b in range(nb)}
     it = {}
-    ret_es = None
     y_own = [None]
 
     def do_S(i, b, ck, deps):
@@ -260,8 +287,8 @@ def rank_program(g, core, T, topo):
         if first:
             run[b]["l"], run[b]["t_l"] = d["ls"], tok[("exp", i)]
         else:
-            d["t_D"] = emit("ve", [d["t_al"], t_id, tok.get(("pv", i - ND))],
-                            lambda: g.vector.tensor_scalar(col(T.D, i % ND), T.ident[:], d["al"], None, Alu.mult))
+            d["t_D"] = emit("se", [d["t_al"], t_id, tok.get(("pv", i - ND))],
+                            lambda: g.scalar.activation(col(T.D, i % ND), T.ident[:], Act.Copy, scale=d["al"]))
             ln, lo = newcol(), run[b]["l"]
             t = emit("ve", [d["t_al"], tok[("exp", i)], run[b]["t_l"]],
                      lambda: g.vector.tensor_scalar(ln, lo, d["al"], d["ls"], Alu.mult, Alu.add))
@@ -288,7 +315,7 @@ def rank_program(g, core, T, topo):
     def do_OUT(i, b, last):
         src = Ob[i % 2][:, 0:B]
         if not last:
-            t = emit("ve", [tok[("pv", i)]], lambda: g.vector.tensor_copy(col(T.Orun, b), src))
+            t = emit("se", [tok[("pv", i)]], lambda: g.scalar.activation(col(T.Orun, b), src, Act.Copy))
             run[b]["t_O"] = t
         else:
             own = loc[b] == core
@@ -297,48 +324,63 @@ def rank_program(g, core, T, topo):
             if own:
                 y_own[0] = t
             else:
-                es = _bits(topo.mask(core, loc[b]))[0::2]
+                m = topo.mask(core, loc[b])
                 rid, pid, _se = topo.addr(loc[b])
                 need("gp", [t])
-                g.remote_dma(col(T.Y, h), col(T.Yo, b), T.sem.yarr, T.sem.snd, pid, rid, _mask(es))
-                sent[0] += len(es)
+                g.remote_dma(col(T.Y, h), col(T.Yo, b), T.sem["yarr%d" % (h // HG)], T.sem.snd, pid, rid, m)
+                sent[0] += len(_bits(m))
         tok[("out", i)] = t
 
+    away = [b for b in order if loc[b] != core]
+    mine = [b for b in order if loc[b] == core]
+    segs = [[(s, b) for b in away] for s in range(nst)]
+    segs[0] = segs[0] + [(0, b) for b in mine]
+    segs[-1] = segs[-1] + [(s, b) for b in mine for s in range(1, nst)]
     i0 = 0
-    for s, (ck, deps) in enumerate(stages):
-        first, last = s == 0, s == len(stages) - 1
+    for seg in segs:
+        n = len(seg)
 
         def head(j):
-            do_S(i0 + j, order[j], ck, deps)
-            do_MAX(i0 + j, order[j], ck, first)
-            do_EXP(i0 + j, order[j], ck, first)
+            s, b = seg[j]
+            do_S(i0 + j, b, stages[s][0], stages[s][1])
+            do_MAX(i0 + j, b, stages[s][0], s == 0)
+            do_EXP(i0 + j, b, stages[s][0], s == 0)
 
         def mid(j):
-            do_T(i0 + j, ck)
-            do_PRE(i0 + j, order[j], first, last)
-            do_CP(i0 + j, ck)
+            s, b = seg[j]
+            do_T(i0 + j, stages[s][0])
+            do_PRE(i0 + j, b, s == 0, s == nst - 1)
+            do_CP(i0 + j, stages[s][0])
 
         def tail(j):
-            do_PV(i0 + j, order[j], ck, first)
-            do_OUT(i0 + j, order[j], last)
+            s, b = seg[j]
+            do_PV(i0 + j, b, stages[s][0], s == 0)
+            do_OUT(i0 + j, b, s == nst - 1)
 
-        for j in range(min(NS, nb)):
+        for j in range(min(NS, n)):
             head(j)
-        for j in range(nb):
+        while later:
+            gi = later.pop(0)
+            carrier_regroup(gi)
+            cross(gi)
+        for j in range(n):
             mid(j)
-            if j + NS < nb:
+            if j + NS < n:
                 head(j + NS)
             if j >= 1:
                 tail(j - 1)
-        tail(nb - 1)
-        i0 += nb
+        tail(n - 1)
+        i0 += n
 
     if is_rank:
-        ny = sum(len(_bits(topo.mask(w, core))[0::2]) for w in members if w != core)
-        expect["yarr"] = ny
-        need("sy", [("yarr", ny), y_own[0]])
-        g.sync.dma_start(T.y[:], T.Y[:]).then_inc(T.sem.st, 16)
-        expect["st"] = 16
+        for gi in range(NG):
+            ws = [members[hh] for hh in range(HG * gi, HG * gi + HG)]
+            ny = sum(len(_bits(topo.mask(w, core))) for w in ws if w != core)
+            expect["yarr%d" % gi] = ny
+            qn = "sy" if gi % 2 == 0 else "se"
+            need(qn, [("yarr%d" % gi, ny)] + ([y_own[0]] if core in ws else []))
+            queues[qn].dma_start(col(T.y, gi, GB), col(T.Y, gi, GB)).then_inc(T.sem["st%d" % gi], 16)
+            expect["st%d" % gi] = 16
 
     expect["snd"] = sent[0]
     expect.update(cnt)

@@ -18,8 +18,9 @@ SCRATCH = {
     "ident": ("sbuf", [128, B], "bfloat16"),
     "P": ("sbuf", [128, NP * 512], "bfloat16"),
     "PTs": ("sbuf", [128, NT * 512], "bfloat16"),
-    "D": ("sbuf", [128, ND * B], "bfloat16"),
-    "Orun": ("sbuf", [128, 4 * B], "bfloat16"),
+    "Os": ("sbuf", [128, ND * B], "float32"),
+    "Tm": ("sbuf", [128, 2 * B], "float32"),
+    "Orun": ("sbuf", [128, 4 * B], "float32"),
     "Yo": ("sbuf", [128, 4 * B], "bfloat16"),
     "Y": ("sbuf", [128, NH * B], "bfloat16"),
     "ST": ("sbuf", [128, 96], "float32"),
@@ -121,8 +122,10 @@ def rank_program(g, core, T, topo):
             (g.sync if n % 2 == 0 else g.scalar).dma_start(o, i).then_inc(T.sem[s], 16)
             expect[s] = 16
 
-    t_ones = emit("ve", [], lambda: g.vector.memset(T.ones[:], 1.0))
-    t_id = emit("gp", [t_ones], lambda: g.affine_select(T.ident[:], T.ones[:], [[-1, B]], Alu.is_equal, 0.0, 0, 1))
+    t_zero = emit("ve", [], lambda: g.vector.memset(T.ones[:], 0.0))
+    t_ones = emit("se", [t_zero], lambda: g.scalar.activation(T.ones[:], T.ones[:], Act.Exp))
+    mk_id = lambda: emit("gp", [t_ones], lambda: g.affine_select(T.ident[:], T.ones[:], [[-1, B]], Alu.is_equal, 0.0, 0, 1))
+    t_id = None if is_rank else mk_id()
 
     def scatter_masks(src, gi):
         ds = [members[hh] for hh in range(HG * gi, HG * gi + HG) if members[hh] != src]
@@ -199,6 +202,8 @@ def rank_program(g, core, T, topo):
                 cross(gi)
             else:
                 later.append(gi)
+    if is_rank:
+        t_id = mk_id()
 
     nL = sum(len(scatter_masks(r, h // HG)[core]) for r in loc if r != core)
     far_d = [r for r in far_loc if carrier[r] == r]
@@ -244,6 +249,8 @@ def rank_program(g, core, T, topo):
     run = {b: {} for b in range(nb)}
     it = {}
     y_own = [None]
+    fc = [0]
+    LF, RF = 80, 88
 
     def do_S(i, b, ck, deps):
         for c, (k, _v) in enumerate(ck):
@@ -254,7 +261,8 @@ def rank_program(g, core, T, topo):
         w = B * len(ck)
         nm = newcol()
         t = emit("ve", [tok[("S", i)]], lambda: g.vector.tensor_reduce(nm, Sb[i % NS][:, 0:w], AxisListType.X, Alu.max, negate=True))
-        d = {"old": None}
+        d = {"old": None, "prev": run[b].get("cur")}
+        run[b]["cur"] = i
         if not first:
             ng = newcol()
             old = run[b]["ng"]
@@ -282,20 +290,29 @@ def rank_program(g, core, T, topo):
                      lambda: g.tensor.transpose(col(PTp[i % 2], c), col(T.P, 4 * (i % NP) + c), T.ident[:]))
         tok[("T", i)] = t
 
-    def do_PRE(i, b, first, last):
+    def do_RESCALE(i, b):
+        d = it[i]
+        d["t_Os"] = emit("se", [d["t_al"], run[b]["t_O"], tok.get(("out", i - ND))],
+                         lambda: g.scalar.activation(col(T.Os, i % ND), col(T.Orun, b), Act.Copy, scale=d["al"]))
+
+    def do_L(i, b, first, ln=None):
         d = it[i]
         if first:
             run[b]["l"], run[b]["t_l"] = d["ls"], tok[("exp", i)]
         else:
-            d["t_D"] = emit("se", [d["t_al"], t_id, tok.get(("pv", i - ND))],
-                            lambda: g.scalar.activation(col(T.D, i % ND), T.ident[:], Act.Copy, scale=d["al"]))
-            ln, lo = newcol(), run[b]["l"]
+            ln, lo = (newcol() if ln is None else ln), run[b]["l"]
             t = emit("ve", [d["t_al"], tok[("exp", i)], run[b]["t_l"]],
                      lambda: g.vector.tensor_scalar(ln, lo, d["al"], d["ls"], Alu.mult, Alu.add))
             run[b]["l"], run[b]["t_l"] = ln, t
-        if last:
-            d["rl"] = newcol()
-            d["t_rl"] = emit("ve", [run[b]["t_l"]], lambda: g.vector.reciprocal(d["rl"], run[b]["l"]))
+
+    def do_FIN(us):
+        k0, k1 = fc[0], fc[0] + len(us)
+        fc[0] = k1
+        for n, (i, b) in enumerate(us):
+            do_L(i, b, False, T.ST[:, LF + k0 + n:LF + k0 + n + 1])
+        t = emit("ve", [run[b]["t_l"] for _i, b in us], lambda: g.vector.reciprocal(T.ST[:, RF + k0:RF + k1], T.ST[:, LF + k0:LF + k1]))
+        for n, (i, b) in enumerate(us):
+            it[i]["rl"], it[i]["t_rl"] = T.ST[:, RF + k0 + n:RF + k0 + n + 1], t
 
     def do_CP(i, ck):
         w = B * len(ck)
@@ -306,21 +323,27 @@ def rank_program(g, core, T, topo):
     def do_PV(i, b, ck, first):
         out = Ob[i % 2][:, 0:B]
         deps = [tok[("cp", i)], tok.get(("out", i - 2))]
-        if not first:
-            emit("pe", deps + [it[i]["t_D"], run[b]["t_O"]], lambda: g.tensor.matmul(out, col(T.D, i % ND), col(T.Orun, b), True, False))
+        if not first and "t_Os" not in it[i]:
+            do_RESCALE(i, b)
         for c, (_k, v) in enumerate(ck):
-            t = emit("pe", deps, lambda: g.tensor.matmul(out, col(T.PTs, 4 * (i % NT) + c), v, first and c == 0, c == len(ck) - 1))
+            t = emit("pe", deps, lambda: g.tensor.matmul(out, col(T.PTs, 4 * (i % NT) + c), v, c == 0, c == len(ck) - 1))
         tok[("pv", i)] = t
 
-    def do_OUT(i, b, last):
+    def do_OUT(i, b, first, last):
         src = Ob[i % 2][:, 0:B]
-        if not last:
+        if first:
             t = emit("se", [tok[("pv", i)]], lambda: g.scalar.activation(col(T.Orun, b), src, Act.Copy))
+            run[b]["t_O"] = t
+        elif not last:
+            t = emit("ve", [tok[("pv", i)], it[i]["t_Os"]], lambda: g.vector.tensor_tensor(col(T.Orun, b), src, col(T.Os, i % ND), Alu.add))
             run[b]["t_O"] = t
         else:
             own = loc[b] == core
             o = col(T.Y, h) if own else col(T.Yo, b)
-            t = emit("ve", [tok[("pv", i)], it[i]["t_rl"]], lambda: g.vector.tensor_scalar(o, src, it[i]["rl"], None, Alu.mult))
+            ta = emit("ve", [tok[("pv", i)], it[i]["t_Os"], tok.get(("fin", i - 2))],
+                      lambda: g.vector.tensor_tensor(col(T.Tm, i % 2), src, col(T.Os, i % ND), Alu.add))
+            t = emit("se", [ta, it[i]["t_rl"]], lambda: g.scalar.activation(o, col(T.Tm, i % 2), Act.Copy, scale=it[i]["rl"]))
+            tok[("fin", i)] = t
             if own:
                 y_own[0] = t
             else:
@@ -329,6 +352,7 @@ def rank_program(g, core, T, topo):
                 need("gp", [t])
                 g.remote_dma(col(T.Y, h), col(T.Yo, b), T.sem["yarr%d" % (h // HG)], T.sem.snd, pid, rid, m)
                 sent[0] += len(_bits(m))
+            t = ta
         tok[("out", i)] = t
 
     away = [b for b in order if loc[b] != core]
@@ -339,6 +363,7 @@ def rank_program(g, core, T, topo):
     i0 = 0
     for seg in segs:
         n = len(seg)
+        grp = [j for j in range(min(NS, n)) if seg[j][0] == nst - 1]
 
         def head(j):
             s, b = seg[j]
@@ -349,13 +374,20 @@ def rank_program(g, core, T, topo):
         def mid(j):
             s, b = seg[j]
             do_T(i0 + j, stages[s][0])
-            do_PRE(i0 + j, b, s == 0, s == nst - 1)
+            if s > 0 and ("out", it[i0 + j]["prev"]) in tok:
+                do_RESCALE(i0 + j, b)
+            if s < nst - 1:
+                do_L(i0 + j, b, s == 0)
+            elif j not in grp:
+                do_FIN([(i0 + j, b)])
             do_CP(i0 + j, stages[s][0])
 
         def tail(j):
             s, b = seg[j]
+            if grp and j == grp[0]:
+                do_FIN([(i0 + jj, seg[jj][1]) for jj in grp])
             do_PV(i0 + j, b, stages[s][0], s == 0)
-            do_OUT(i0 + j, b, s == nst - 1)
+            do_OUT(i0 + j, b, s == 0, s == nst - 1)
 
         for j in range(min(NS, n)):
             head(j)

from concourse.bass import DstId, RemoteDMATransfer
from concourse.mybir import AluOpType, AxisListType, ActivationFunctionType

NH = 8
B = 128
GW = 3 * B
NG = 2
HG = NH // NG
NS, NP, NT, ND = 4, 4, 3, 4

SCRATCH = {
    "KVn": ("sbuf", [128, 2 * NH * B], "bfloat16"),
    "Qn": ("sbuf", [128, NH * B], "bfloat16"),
    "X": ("sbuf", [128, NH * GW], "bfloat16"),
    "L": ("sbuf", [128, 4 * GW], "bfloat16"),
    "R": ("sbuf", [128, 4 * 2 * B], "bfloat16"),
    "ones": ("sbuf", [128, B], "bfloat16"),
    "ident": ("sbuf", [128, B], "bfloat16"),
    "P": ("sbuf", [128, NP * 512], "bfloat16"),
    "PTs": ("sbuf", [128, NT * 512], "bfloat16"),
    "Os": ("sbuf", [128, ND * B], "float32"),
    "Tm": ("sbuf", [128, 2 * B], "float32"),
    "Orun": ("sbuf", [128, 4 * B], "float32"),
    "Yo": ("sbuf", [128, 4 * B], "bfloat16"),
    "Y": ("sbuf", [128, NH * B], "bfloat16"),
    "ST": ("sbuf", [128, 96], "float32"),
    "S0": ("psum", [128, 512], "float32"),
    "S1": ("psum", [128, 512], "float32"),
    "S2": ("psum", [128, 512], "float32"),
    "S3": ("psum", [128, 512], "float32"),
    "PT0": ("psum", [128, 1024], "bfloat16"),
    "PT1": ("psum", [128, 1024], "bfloat16"),
    "O0": ("psum", [128, 512], "float32"),
    "O1": ("psum", [128, 512], "float32"),
}
SEMAPHORES = ["pe", "ve", "se", "gp", "lk0", "lv0", "lq0", "lk1", "lv1", "lq1", "feed0", "feed1",
              "arrL", "arrD", "arrR", "yarr0", "yarr1", "snd", "st0", "st1"]


def _bits(m):
    return [e for e in range(m.bit_length()) if (m >> e) & 1]


def _mask(es):
    return sum(1 << e for e in es)


def _plan(T, topo):
    ranks = [int(c) for c in T.cores]
    chips = []
    for c in ranks:
        if topo.chip(c) not in chips:
            chips.append(topo.chip(c))
    allc = range(topo.CHIPS * topo.CORES_PER_CHIP)
    members = {ch: [c for c in allc if topo.chip(c) == ch] for ch in chips}
    loc = {ch: [c for c in ranks if topo.chip(c) == ch] for ch in chips}
    other = {chips[0]: chips[1], chips[1]: chips[0]}
    carrier = {}
    for ch in chips:
        far = members[other[ch]][0]
        own_dies = [topo.die(r) for r in loc[ch] if topo.may_write(r, far)]
        free = [c for c in members[ch] if c not in ranks and topo.may_write(c, far)]
        free.sort(key=lambda c: topo.die(c) in own_dies)
        for r in loc[ch]:
            carrier[r] = r if topo.may_write(r, far) else free.pop(0)
    return {"members": members, "loc": loc, "other": other, "carrier": carrier}


def rank_program(g, core, T, topo):
    pl = _plan(T, topo)
    ch = topo.chip(core)
    if ch not in pl["members"]:
        return
    members, loc = pl["members"][ch], pl["loc"][ch]
    far_members, far_loc = pl["members"][pl["other"][ch]], pl["loc"][pl["other"][ch]]
    carrier = pl["carrier"]
    h = members.index(core)
    is_rank = core in loc
    carried = [r for r in loc if carrier[r] == core]
    Act, Alu = ActivationFunctionType, AluOpType

    queues = {"pe": g.tensor, "ve": g.vector, "se": g.scalar, "gp": g, "sy": g.sync}
    cnt = {"pe": 0, "ve": 0, "se": 0, "gp": 0}
    seen = {q: {} for q in queues}
    expect = {}
    sent = [0]

    def need(q, deps):
        for d in deps:
            if d is not None and seen[q].get(d[0], 0) < d[1]:
                queues[q].wait_ge(T.sem[d[0]], d[1])
                seen[q][d[0]] = d[1]

    def emit(q, deps, fn):
        need(q, deps)
        fn().then_inc(T.sem[q], 1)
        cnt[q] += 1
        return (q, cnt[q])

    def dst_id(c):
        rid, pid, _se = topo.addr(c)
        return DstId(rid=rid, pnc=pid)

    def col(t, j, w=B):
        return t[:, j * w:(j + 1) * w]

    X = T.X
    GB = HG * B
    xk = lambda hh: X[:, GW * hh:GW * hh + B]
    xv = lambda hh: X[:, GW * hh + B:GW * hh + 2 * B]
    xq = lambda hh: X[:, GW * hh + 2 * B:GW * hh + 3 * B]
    nk = lambda hh: col(T.KVn, 2 * HG * (hh // HG) + hh % HG)
    nv = lambda hh: col(T.KVn, 2 * HG * (hh // HG) + HG + hh % HG)

    if is_rank:
        jobs = []
        for gi in range(NG):
            jobs.append((T.KVn[:, 2 * GB * gi:2 * GB * gi + GB], col(T.k, gi, GB), "lk%d" % gi))
            jobs.append((T.KVn[:, 2 * GB * gi + GB:2 * GB * gi + 2 * GB], col(T.v, gi, GB), "lv%d" % gi))
            jobs.append((col(T.Qn, gi, GB), col(T.q, gi, GB), "lq%d" % gi))
        for n, (o, i, s) in enumerate(jobs):
            (g.sync if n % 2 == 0 else g.scalar).dma_start(o, i).then_inc(T.sem[s], 16)
            expect[s] = 16

    t_zero = emit("ve", [], lambda: g.vector.memset(T.ones[:], 0.0))
    t_ones = emit("se", [t_zero], lambda: g.scalar.activation(T.ones[:], T.ones[:], Act.Exp))
    mk_id = lambda: emit("gp", [t_ones], lambda: g.affine_select(T.ident[:], T.ones[:], [[-1, B]], Alu.is_equal, 0.0, 0, 1))
    t_id = None if is_rank else mk_id()

    def scatter_masks(src, gi):
        ds = [members[hh] for hh in range(HG * gi, HG * gi + HG) if members[hh] != src]
        pool = _bits(topo.mask(src, ds[0]))
        if gi > 0 and carrier[src] == src:
            out = _bits(topo.mask(src, far_members[0]))
            pool = [e for e in pool if e not in out]
        per = 1
        while per * 2 * len(ds) <= len(pool):
            per *= 2
        return {w: pool[per * i:per * i + per] for i, w in enumerate(ds)}

    off = _bits(topo.mask(core, far_members[0]))
    per_off = len(off) // HG
    il = {}

    def carrier_regroup(gi):
        hs = range(HG * gi, HG * gi + HG)
        fd = ("feed%d" % gi, len(_bits(topo.mask(carried[0], core))))
        expect[fd[0]] = fd[1]
        jobs = [(xk(hh), nk(hh)) for hh in hs] + [(xv(hh), nv(hh)) for hh in hs]
        nve = (2 * len(jobs) + 2) // 3 if gi == 0 else len(jobs)
        ts = None
        for o, i in jobs[:nve]:
            tv = emit("ve", [fd], lambda: g.vector.tensor_copy(o, i))
        for o, i in jobs[nve:]:
            ts = emit("se", [fd], lambda: g.scalar.activation(o, i, Act.Copy))
        il[gi] = [tv, ts]

    def cross(gi):
        need("gp", il[gi])
        r = carried[0]
        b = loc.index(r)
        sem = T.sem.arrD if r == core else T.sem.arrR
        trs = [RemoteDMATransfer(dst_ids=[dst_id(far_members[hh])], dma_engine_mask=_mask(off[per_off * i:per_off * i + per_off]),
                                 remote_sem=sem, src=X[:, GW * hh:GW * hh + 2 * B], dst=col(T.R, b, 2 * B))
               for i, hh in enumerate(range(HG * gi, HG * gi + HG))]
        g.remote_dma_fused(trs, local_sem=T.sem.snd)
        sent[0] += per_off * HG

    later = []
    for gi in range(NG):
        hs = range(HG * gi, HG * gi + HG)
        lk, lv, lq = ("lk%d" % gi, 16), ("lv%d" % gi, 16), ("lq%d" % gi, 16)
        if is_rank and carrier[core] != core:
            c = carrier[core]
            m = topo.mask(core, c)
            rid, pid, _se = topo.addr(c)
            need("gp", [lk, lv])
            g.remote_dma(col(T.KVn, gi, 2 * GB), col(T.KVn, gi, 2 * GB), T.sem["feed%d" % gi], T.sem.snd, pid, rid, m)
            sent[0] += len(_bits(m))
        if is_rank:
            for hh in hs:
                tv = emit("ve", [lk], lambda: g.vector.tensor_copy(xk(hh), nk(hh)))
            for hh in hs:
                tv = emit("ve", [lv], lambda: g.vector.tensor_copy(xv(hh), nv(hh)))
            for hh in hs[:HG // 2]:
                ts = emit("se", [lq], lambda: g.scalar.activation(xq(hh), col(T.Qn, hh), Act.Copy))
            for hh in hs[HG // 2:]:
                tv = emit("ve", [lq], lambda: g.vector.tensor_copy(xq(hh), col(T.Qn, hh)))
            il[gi] = [tv, ts]
            need("gp", il[gi])
            sm = scatter_masks(core, gi)
            b = loc.index(core)
            trs = [RemoteDMATransfer(dst_ids=[dst_id(w)], dma_engine_mask=_mask(es), remote_sem=T.sem.arrL,
                                     src=col(X, members.index(w), GW), dst=col(T.L, b, GW)) for w, es in sm.items()]
            g.remote_dma_fused(trs, local_sem=T.sem.snd)
            sent[0] += sum(len(es) for es in sm.values())
            if carried:
                cross(gi)
        elif carried:
            if gi == 0:
                carrier_regroup(gi)
                cross(gi)
            else:
                later.append(gi)
    if is_rank:
        t_id = mk_id()

    nL = sum(len(scatter_masks(r, h // HG)[core]) for r in loc if r != core)
    far_d = [r for r in far_loc if carrier[r] == r]
    far_r = [r for r in far_loc if carrier[r] != r]
    expect["arrL"] = nL
    expect["arrD"] = per_off * len(far_d)
    expect["arrR"] = per_off * len(far_r)

    q_ap, kv_loc = [], []
    for b, r in enumerate(loc):
        if r == core:
            q_ap.append(xq(h))
            kv_loc.append((xk(h), xv(h)))
        else:
            o = GW * b
            q_ap.append(T.L[:, o + 2 * B:o + 3 * B])
            kv_loc.append((T.L[:, o:o + B], T.L[:, o + B:o + 2 * B]))

    def kv_far(r):
        o = 2 * B * far_loc.index(r)
        return (T.R[:, o:o + B], T.R[:, o + B:o + 2 * B])

    stages = [(kv_loc, [("arrL", nL)] + (il[h // HG] if is_rank else []))]
    far_st = [([kv_far(r) for r in rs], [(s, expect[s])]) for rs, s in ((far_d, "arrD"), (far_r, "arrR")) if rs]
    if is_rank:
        stages += far_st
    else:
        stages.append((sum([c for c, _d in far_st], []), sum([d for _c, d in far_st], [])))
    nst = len(stages)

    nb = len(loc)
    order = [(h + 1 + j) % nb for j in range(nb)]
    Sb = [T.S0, T.S1, T.S2, T.S3]
    PTp = [T.PT0, T.PT1]
    Ob = [T.O0, T.O1]
    stc = [0]

    def newcol():
        stc[0] += 1
        return T.ST[:, stc[0] - 1:stc[0]]

    tok = {}
    run = {b: {} for b in range(nb)}
    it = {}
    y_own = [None]
    fc = [0]
    LF, RF = 80, 88

    def do_S(i, b, ck, deps):
        for c, (k, _v) in enumerate(ck):
            t = emit("pe", deps + [tok.get(("exp", i - NS))], lambda: g.tensor.matmul(col(Sb[i % NS], c), q_ap[b], k, True, True))
        tok[("S", i)] = t

    def do_MAX(i, b, ck, first):
        w = B * len(ck)
        nm = newcol()
        t = emit("ve", [tok[("S", i)]], lambda: g.vector.tensor_reduce(nm, Sb[i % NS][:, 0:w], AxisListType.X, Alu.max, negate=True))
        d = {"old": None, "prev": run[b].get("cur")}
        run[b]["cur"] = i
        if not first:
            ng = newcol()
            old = run[b]["ng"]
            t = emit("ve", [t, run[b]["t_ng"]], lambda: g.vector.tensor_tensor(ng, nm, old, Alu.min))
            d["old"] = old
            nm = ng
        d["ng"] = nm
        run[b]["ng"], run[b]["t_ng"] = nm, t
        it[i] = d

    def do_EXP(i, b, ck, first):
        w = B * len(ck)
        d = it[i]
        if not first:
            d["al"] = newcol()
            d["t_al"] = emit("se", [run[b]["t_ng"]], lambda: g.scalar.activation(d["al"], d["old"], Act.Exp, bias=d["ng"], scale=-1.0))
        d["ls"] = newcol()
        p = T.P[:, 512 * (i % NP):512 * (i % NP) + w]
        tok[("exp", i)] = emit("se", [run[b]["t_ng"], tok.get(("T", i - NP))],
                               lambda: g.scalar.activation(p, Sb[i % NS][:, 0:w], Act.Exp, bias=d["ng"], scale=1.0, accum_out=d["ls"]))

    def do_T(i, ck):
        for c in range(len(ck)):
            t = emit("pe", [tok[("exp", i)], tok.get(("cp", i - 2)), t_id],
                     lambda: g.tensor.transpose(col(PTp[i % 2], c), col(T.P, 4 * (i % NP) + c), T.ident[:]))
        tok[("T", i)] = t

    def do_RESCALE(i, b):
        d = it[i]
        d["t_Os"] = emit("se", [d["t_al"], run[b]["t_O"], tok.get(("out", i - ND))],
                         lambda: g.scalar.activation(col(T.Os, i % ND), col(T.Orun, b), Act.Copy, scale=d["al"]))

    def do_L(i, b, first, ln=None):
        d = it[i]
        if first:
            run[b]["l"], run[b]["t_l"] = d["ls"], tok[("exp", i)]
        else:
            ln, lo = (newcol() if ln is None else ln), run[b]["l"]
            t = emit("ve", [d["t_al"], tok[("exp", i)], run[b]["t_l"]],
                     lambda: g.vector.tensor_scalar(ln, lo, d["al"], d["ls"], Alu.mult, Alu.add))
            run[b]["l"], run[b]["t_l"] = ln, t

    def do_FIN(us):
        k0, k1 = fc[0], fc[0] + len(us)
        fc[0] = k1
        for n, (i, b) in enumerate(us):
            do_L(i, b, False, T.ST[:, LF + k0 + n:LF + k0 + n + 1])
        t = emit("ve", [run[b]["t_l"] for _i, b in us], lambda: g.vector.reciprocal(T.ST[:, RF + k0:RF + k1], T.ST[:, LF + k0:LF + k1]))
        for n, (i, b) in enumerate(us):
            it[i]["rl"], it[i]["t_rl"] = T.ST[:, RF + k0 + n:RF + k0 + n + 1], t

    def do_CP(i, ck):
        w = B * len(ck)
        o = 512 * (i % NT)
        tok[("cp", i)] = emit("ve", [tok[("T", i)], tok.get(("pv", i - NT))],
                              lambda: g.vector.tensor_copy(T.PTs[:, o:o + w], PTp[i % 2][:, 0:w]))

    def do_PV(i, b, ck, first):
        out = Ob[i % 2][:, 0:B]
        deps = [tok[("cp", i)], tok.get(("out", i - 2))]
        if not first and "t_Os" not in it[i]:
            do_RESCALE(i, b)
        for c, (_k, v) in enumerate(ck):
            t = emit("pe", deps, lambda: g.tensor.matmul(out, col(T.PTs, 4 * (i % NT) + c), v, c == 0, c == len(ck) - 1))
        tok[("pv", i)] = t

    def do_OUT(i, b, first, last):
        src = Ob[i % 2][:, 0:B]
        if first:
            t = emit("se", [tok[("pv", i)]], lambda: g.scalar.activation(col(T.Orun, b), src, Act.Copy))
            run[b]["t_O"] = t
        elif not last:
            t = emit("ve", [tok[("pv", i)], it[i]["t_Os"]], lambda: g.vector.tensor_tensor(col(T.Orun, b), src, col(T.Os, i % ND), Alu.add))
            run[b]["t_O"] = t
        else:
            own = loc[b] == core
            o = col(T.Y, h) if own else col(T.Yo, b)
            ta = emit("ve", [tok[("pv", i)], it[i]["t_Os"], tok.get(("fin", i - 2))],
                      lambda: g.vector.tensor_tensor(col(T.Tm, i % 2), src, col(T.Os, i % ND), Alu.add))
            t = emit("se", [ta, it[i]["t_rl"]], lambda: g.scalar.activation(o, col(T.Tm, i % 2), Act.Copy, scale=it[i]["rl"]))
            tok[("fin", i)] = t
            if own:
                y_own[0] = t
            else:
                m = topo.mask(core, loc[b])
                rid, pid, _se = topo.addr(loc[b])
                need("gp", [t])
                g.remote_dma(col(T.Y, h), col(T.Yo, b), T.sem["yarr%d" % (h // HG)], T.sem.snd, pid, rid, m)
                sent[0] += len(_bits(m))
            t = ta
        tok[("out", i)] = t

    away = [b for b in order if loc[b] != core]
    mine = [b for b in order if loc[b] == core]
    segs = [[(s, b) for b in away] for s in range(nst)]
    segs[0] = segs[0] + [(0, b) for b in mine]
    segs[-1] = segs[-1] + [(s, b) for b in mine for s in range(1, nst)]
    i0 = 0
    for seg in segs:
        n = len(seg)
        grp = [j for j in range(min(NS, n)) if seg[j][0] == nst - 1]

        def head(j):
            s, b = seg[j]
            do_S(i0 + j, b, stages[s][0], stages[s][1])
            do_MAX(i0 + j, b, stages[s][0], s == 0)
            do_EXP(i0 + j, b, stages[s][0], s == 0)

        def mid(j):
            s, b = seg[j]
            do_T(i0 + j, stages[s][0])
            if s > 0 and ("out", it[i0 + j]["prev"]) in tok:
                do_RESCALE(i0 + j, b)
            if s < nst - 1:
                do_L(i0 + j, b, s == 0)
            elif j not in grp:
                do_FIN([(i0 + j, b)])
            do_CP(i0 + j, stages[s][0])

        def tail(j):
            s, b = seg[j]
            if grp and j == grp[0]:
                do_FIN([(i0 + jj, seg[jj][1]) for jj in grp])
            do_PV(i0 + j, b, stages[s][0], s == 0)
            do_OUT(i0 + j, b, s == 0, s == nst - 1)

        for j in range(min(NS, n)):
            head(j)
        while later:
            gi = later.pop(0)
            carrier_regroup(gi)
            cross(gi)
        for j in range(n):
            mid(j)
            if j + NS < n:
                head(j + NS)
            if j >= 1:
                tail(j - 1)
        tail(n - 1)
        i0 += n

    if is_rank:
        for gi in range(NG):
            ws = [members[hh] for hh in range(HG * gi, HG * gi + HG)]
            ny = sum(len(_bits(topo.mask(w, core))) for w in ws if w != core)
            expect["yarr%d" % gi] = ny
            qn = "sy" if gi % 2 == 0 else "se"
            need(qn, [("yarr%d" % gi, ny)] + ([y_own[0]] if core in ws else []))
            queues[qn].dma_start(col(T.y, gi, GB), col(T.Y, gi, GB)).then_inc(T.sem["st%d" % gi], 16)
            expect["st%d" % gi] = 16

    expect["snd"] = sent[0]
    expect.update(cnt)
    need("gp", [(s, n) for s, n in expect.items() if n > 0])
